import numpy as np
import ml_dtypes


def mxq(x, axis, fmt="e4m3"):
    dtype, down = {"e4m3": (ml_dtypes.float8_e4m3fn, 7), "e5m2": (ml_dtypes.float8_e5m2, 14)}[fmt]
    v = np.moveaxis(np.asarray(x, np.float32).astype(ml_dtypes.bfloat16).astype(np.float64), axis, -1)
    blocks = v.reshape(v.shape[:-1] + (-1, 32))
    amax = np.abs(blocks).max(-1, keepdims=True)
    byte = np.maximum(np.where(amax > 0, np.frexp(amax)[1] - 1 + 127, 0) - down, 1)
    scale = np.exp2(byte - 127.0)
    codes = (blocks / scale).astype(np.float32).astype(dtype).astype(np.float64)
    return np.moveaxis((codes * scale).reshape(v.shape), -1, axis)


WIDE = False


def mx_kscale(k):
    if not WIDE:
        return np.ones(k)
    levels = np.array([24, -24, 12, -12, 0])
    if k % 512:
        return np.exp2(np.random.permutation(np.resize(levels, k // 32))).repeat(32)
    a = np.empty((k // 512, 16))
    for p in range(k // 512):
        a[p, :8] = np.random.permutation(np.resize(levels, 8))
        for g in range(8):
            far = levels[np.abs(levels - a[p, g]) >= 10]
            a[p, g + 8] = far[np.random.randint(len(far))]
    return np.exp2(a.ravel()).repeat(32)


def f64(x):
    return np.asarray(x).astype(np.float64)


def striped8(idx):
    return np.concatenate([v.reshape(-1, 16).T for v in idx]).astype(np.uint16)


def unstriped8(offs):
    return np.stack([offs[16 * g:16 * g + 16].T.reshape(-1) for g in range(8)]).astype(np.int64)


E2M1 = np.array([0.0, 0.5, 1.0, 1.5, 2.0, 3.0, 4.0, 6.0, -0.0, -0.5, -1.0, -1.5, -2.0, -3.0, -4.0, -6.0])


def pack_weight(w, fmt):
    k, n = w.shape
    w = f64(np.asarray(w, np.float32).astype(ml_dtypes.bfloat16)).reshape(k // 32, 32, n)
    amax = np.abs(w).max(1)
    if fmt == "e4m3":
        byte = np.frexp(amax)[1] - 1 + 127 - 7
    else:
        mant, ex = np.frexp(amax / 6.0)
        byte = np.where(mant > 0.5, ex, ex - 1) + 127
    byte = np.clip(np.where(amax > 0, byte, 1), 1, 254)
    scaled = (w * np.exp2(127.0 - byte)[:, None, :]).reshape(k, n).astype(np.float32)
    by_word = np.ascontiguousarray(scaled.reshape(k // 512, 128, 4, n).transpose(0, 1, 3, 2))
    if fmt == "e4m3":
        words = by_word.astype(ml_dtypes.float8_e4m3fn).view(np.uint8)
    else:
        c = by_word.astype(ml_dtypes.float4_e2m1fn).view(np.uint8) & 0xF
        words = (c[..., 0::2] | (c[..., 1::2] << 4)).reshape(k // 512, 128, 2 * n)
    return np.ascontiguousarray(words), np.ascontiguousarray(byte.astype(np.uint8).reshape(k // 512, 16, n))


def unpack_weight(words, scales, fmt):
    g, _, n = scales.shape
    words = np.ascontiguousarray(words).reshape(g, 128, n, -1)
    if fmt == "e4m3":
        vals = words.view(ml_dtypes.float8_e4m3fn).astype(np.float64)
    else:
        nib = np.empty((g, 128, n, 4), np.uint8)
        nib[..., 0::2] = words & 0xF
        nib[..., 1::2] = words >> 4
        vals = E2M1[nib]
    vals = vals * np.repeat(np.exp2(scales.astype(np.float64) - 127.0), 8, axis=1)[..., None]
    return vals.transpose(0, 1, 3, 2).reshape(g * 512, n)


def planes(y):
    n, m = y.shape
    v = y.astype(np.float32).astype(ml_dtypes.bfloat16).astype(np.float64).reshape(n // 32, 32, m)
    top = np.abs(v).max(1)
    byte = np.clip(np.where(top > 0, np.frexp(top)[1] - 1 + 127 - 7, 1), 1, 254)
    codes = (v * np.exp2(127.0 - byte)[:, None, :]).reshape(n, m).astype(np.float32).astype(ml_dtypes.float8_e4m3fn).view(np.uint8)
    words = codes.reshape(n // 512, 128, 4, m).transpose(0, 1, 3, 2)
    return np.ascontiguousarray(words), np.ascontiguousarray(byte.astype(np.uint8).reshape(n // 512, 16, m))


K, L, N, T, J = 512, 512, 512, 2048, 1024


def setup_inputs():
    n = np.random.standard_normal
    s = mx_kscale(K)[:, None]
    s2 = mx_kscale(L)[:, None]
    p_wb = pack_weight(n((L, N)) / np.sqrt(L) / s2, "e2m1")
    return {
        "xT": (n((K, T)) * s).astype(np.float32),
        "wgt": np.repeat(np.random.uniform(0.5, 2.0, (8, J)), 16, axis=0).astype(np.float32),
        "zT": (n((L, T)) * s2).astype(np.float32),
        "wgt2": np.repeat(np.random.uniform(0.5, 2.0, (8, J)), 16, axis=0).astype(np.float32),
        "wa": (n((K, N)) / np.sqrt(K) / s).astype(np.float32),
        "wb_words": p_wb[0],
        "wb_scales": p_wb[1],
        "b": (0.3 * n(N)).astype(np.float32),
        "offs": striped8(np.stack([np.random.permutation(T)[:J] for _ in range(8)])),
        "offs2": striped8(np.stack([np.random.permutation(T)[:J] for _ in range(8)])),
    }


def reference(xT, wgt, zT, wgt2, wa, wb_words, wb_scales, b, offs, offs2):
    idx = unstriped8(offs)
    idx2 = unstriped8(offs2)
    rows = np.arange(K)
    xg = f64(wgt)[rows // 4 % 128] * f64(xT)[rows[:, None], idx[rows % 512 // 64]]
    xT_ = mxq(xg, 0, "e4m3")
    rows = np.arange(L)
    xg = f64(wgt2)[rows // 4 % 128] * f64(zT)[rows[:, None], idx2[rows % 512 // 64]]
    zT_ = mxq(xg, 0, "e4m3")
    wa_ = mxq(f64(wa), 0, "e4m3")
    wb_ = unpack_weight(wb_words, wb_scales, "e2m1")
    ya = wa_.T @ xT_
    yb = wb_.T @ zT_
    out_0 = np.abs(ya - yb) + f64(b)[:, None]
    return (out_0,) + planes(out_0)

@@ -1,0 +1,196 @@
+from contextlib import ExitStack
+
+import concourse.mybir as mybir
+
+K, L, N, T, J = 512, 512, 512, 2048, 1024
+FLOPS = 2 * (K + L) * N * J
+
+F32 = mybir.dt.float32
+BF16 = mybir.dt.bfloat16
+I32 = mybir.dt.int32
+U32 = mybir.dt.uint32
+U16 = mybir.dt.uint16
+U8 = mybir.dt.uint8
+FP8X4 = mybir.dt.float8_e4m3fn_x4
+FP4X4 = mybir.dt.float4_e2m1fn_x4
+MULT = mybir.AluOpType.mult
+ACT = mybir.ActivationFunctionType
+
+P = 128
+PACK = 4
+LANES = 16
+CHUNK = 256
+CHUNKS = J // CHUNK
+HALF = J // 2
+FP4_N = 128
+
+
+def tile_list_absd_biasP_kernel(
+    tc, xT, wgt, zT, wgt2, wa, wb_words, wb_scales, b, offs, offs2, out_0, out_1, out_2
+):
+    nc = tc.nc
+    with ExitStack() as ctx:
+        keep = ctx.enter_context(tc.tile_pool(name="keep", bufs=1))
+        psum = ctx.enter_context(tc.psum_pool(name="psum", bufs=1))
+
+        def interleave(copy, grouped, planes):
+            copy(
+                grouped.rearrange("p (c i) t -> p c t i", i=PACK),
+                planes.rearrange("p t (c i) -> p c t i", i=PACK),
+            )
+
+        def quantize(codes, scales, grouped):
+            nc.vector.quantize_mx(
+                out=codes.bitcast(FP8X4), scales=scales, in_=grouped.rearrange("p j t -> p (j t)")
+            )
+
+        x_rows = xT.rearrange("(p i) t -> p i t", i=PACK)
+        z_rows = zT.rearrange("(p i) t -> p i t", i=PACK)
+        x_list = keep.tile([P, J // LANES], U16, name="x_list")
+        z_list = keep.tile([P, J // LANES], U16, name="z_list")
+        x_plane = [keep.tile([P, T], F32, name="x_plane%d" % i) for i in range(PACK)]
+        z_plane = [keep.tile([P, T], F32, name="z_plane%d" % i) for i in range(PACK)]
+        x_wgt = keep.tile([P, J], F32, name="x_wgt")
+        z_wgt = keep.tile([P, J], F32, name="z_wgt")
+        wa_raw = keep.tile([P, PACK, N], F32, name="wa_raw")
+        wb_raw = keep.tile([P, 2 * N], U8, name="wb_raw")
+        wb_scale_raw = keep.tile([P, N], U8, name="wb_scale_raw")
+        bias = keep.tile([P, PACK], F32, name="bias")
+
+        nc.sync.dma_start(x_list[:], offs)
+        nc.sync.dma_start(x_plane[0][:], x_rows[:, 0, :])
+        nc.sync.dma_start(x_wgt[:, :HALF], wgt[:, :HALF])
+        nc.sync.dma_start(x_wgt[:, HALF:], wgt[:, HALF:])
+        nc.sync.dma_start(wb_raw[:].bitcast(I32), wb_words[0].bitcast(I32))
+        nc.gpsimd.memset(wb_scale_raw[:].bitcast(I32), 0)
+        for q in range(4):
+            nc.gpsimd.dma_start(
+                wb_scale_raw[32 * q : 32 * q + 4, :].bitcast(I32), wb_scales[0, 4 * q : 4 * q + 4, :].bitcast(I32)
+            )
+        nc.gpsimd.dma_start(bias[:], b.rearrange("(p t) -> p t", t=PACK))
+        for i in range(1, PACK):
+            nc.sync.dma_start(x_plane[i][:], x_rows[:, i, :])
+        nc.sync.dma_start(z_list[:], offs2)
+        nc.sync.dma_start(z_wgt[:], wgt2)
+        nc.sync.dma_start(z_plane[0][:], z_rows[:, 0, :])
+        nc.sync.dma_start(z_plane[1][:], z_rows[:, 1, :])
+        nc.sync.dma_start(wa_raw[:], wa.rearrange("(p i) n -> p i n", i=PACK))
+        nc.sync.dma_start(z_plane[2][:], z_rows[:, 2, :])
+        nc.sync.dma_start(z_plane[3][:], z_rows[:, 3, :])
+
+        def gather(picked, plane, lists, weights, i, j0, j1):
+            nc.vector.tensor_tensor(
+                picked[:, i, j0:j1],
+                plane[i][:].indirect(lists[:, j0 // LANES : j1 // LANES]),
+                weights[:, j0:j1],
+                MULT,
+            )
+
+        x_picked = keep.tile([P, PACK, J], F32, name="x_picked")
+        z_picked = keep.tile([P, PACK, J], F32, name="z_picked")
+        x_grouped = keep.tile([P, J, PACK], BF16, name="x_grouped", align_bytes=64)
+        z_grouped = keep.tile([P, J, PACK], BF16, name="z_grouped", align_bytes=64)
+        x_codes = keep.tile([P, J], U32, name="x_codes", align_bytes=64)
+        z_codes = keep.tile([P, J], U32, name="z_codes", align_bytes=64)
+        x_scales = keep.tile([P, J], U8, name="x_scales", align_bytes=64)
+        z_scales = keep.tile([P, J], U8, name="z_scales", align_bytes=64)
+
+        gather(x_picked, x_plane, x_list, x_wgt, 0, 0, HALF)
+        gather(x_picked, x_plane, x_list, x_wgt, 0, HALF, J)
+        gather(x_picked, x_plane, x_list, x_wgt, 1, 0, J)
+
+        wb_codes = keep.tile([P, PACK, 2 * P], U8, name="wb_codes", align_bytes=64)
+        wb_scale = keep.tile([P, PACK, P], U8, name="wb_scale", align_bytes=64)
+        nc.vector.tensor_copy(
+            wb_codes[:].rearrange("p t (m e) -> p t m e", e=2),
+            wb_raw[:].rearrange("p (m t e) -> p t m e", t=PACK, e=2),
+        )
+        nc.vector.tensor_copy(wb_scale[:], wb_scale_raw[:].rearrange("p (m t) -> p t m", t=PACK))
+
+        gather(x_picked, x_plane, x_list, x_wgt, 2, 0, J)
+        gather(x_picked, x_plane, x_list, x_wgt, 3, 0, HALF)
+        gather(x_picked, x_plane, x_list, x_wgt, 3, HALF, J)
+        for j0 in (0, HALF):
+            interleave(nc.scalar.copy, x_grouped[:, j0 : j0 + HALF, :], x_picked[:, :, j0 : j0 + HALF])
+        gather(z_picked, z_plane, z_list, z_wgt, 0, 0, J)
+        gather(z_picked, z_plane, z_list, z_wgt, 1, 0, J)
+        for j0 in (0, HALF):
+            quantize(x_codes[:, j0 : j0 + HALF], x_scales[:, j0 : j0 + HALF], x_grouped[:, j0 : j0 + HALF, :])
+
+        wa_grouped = keep.tile([P, N, PACK], BF16, name="wa_grouped", align_bytes=64)
+        wa_codes = keep.tile([P, N], U32, name="wa_codes", align_bytes=64)
+        wa_scales = keep.tile([P, N], U8, name="wa_scales", align_bytes=64)
+        nc.scalar.activation(
+            wa_grouped[:].rearrange("p (t m) i -> p m i t", t=PACK),
+            wa_raw[:].rearrange("p i (m t) -> p m i t", t=PACK),
+            ACT.Copy,
+            scale=-1.0,
+        )
+        gather(z_picked, z_plane, z_list, z_wgt, 2, 0, J)
+        quantize(wa_codes[:], wa_scales[:], wa_grouped[:])
+
+        banks = [[psum.tile([P, 2, CHUNK], F32, name="bank%d_%d" % (c, h)) for h in range(2)] for c in range(CHUNKS)]
+        for c in range(CHUNKS):
+            cols = slice(c * CHUNK, (c + 1) * CHUNK)
+            for t in range(PACK):
+                nc.tensor.matmul_mx(
+                    out=banks[c][t // 2][:, t % 2, :],
+                    lhsT=wa_codes[:, t * P : (t + 1) * P].bitcast(FP8X4),
+                    lhsT_scale=wa_scales[:, t * P : (t + 1) * P],
+                    rhs=x_codes[:, cols].bitcast(FP8X4),
+                    rhs_scale=x_scales[:, cols],
+                    start=(t % 2 == 0),
+                    stop=False,
+                )
+
+        y_codes = keep.tile([P, J], U32, name="y_codes", align_bytes=64)
+        y_scales = keep.tile([P, J], U8, name="y_scales", align_bytes=64)
+        y_rows = out_0.rearrange("(p t) j -> p t j", t=PACK)
+        y_words = out_1[0].rearrange("p j i -> p (j i)").bitcast(I32)
+
+        def front(c):
+            cols = slice(c * CHUNK, (c + 1) * CHUNK)
+            interleave(nc.scalar.copy, z_grouped[:, cols, :], z_picked[:, :, cols])
+            quantize(z_codes[:, cols], z_scales[:, cols], z_grouped[:, cols, :])
+            for t in range(PACK):
+                for s in range(CHUNK // FP4_N):
+                    part = slice(c * CHUNK + s * FP4_N, c * CHUNK + (s + 1) * FP4_N)
+                    nc.tensor.matmul_mx(
+                        out=banks[c][t // 2][:, t % 2, s * FP4_N : (s + 1) * FP4_N],
+                        lhsT=wb_codes[:, t, :].bitcast(FP4X4),
+                        lhsT_scale=wb_scale[:, t, :],
+                        rhs=z_codes[:, part].bitcast(FP8X4),
+                        rhs_scale=z_scales[:, part],
+                        start=False,
+                        stop=(t % 2 == 1 and s == CHUNK // FP4_N - 1),
+                    )
+
+        def back(c):
+            cols = slice(c * CHUNK, (c + 1) * CHUNK)
+            dist = keep.tile([P, PACK, CHUNK], F32, name="dist%d" % c)
+            y = keep.tile([P, PACK, CHUNK], F32, name="y%d" % c)
+            y_grouped = keep.tile([P, CHUNK, PACK], BF16, name="y_grouped%d" % c, align_bytes=64)
+            for h in range(2):
+                nc.scalar.activation(dist[:, 2 * h : 2 * h + 2, :], banks[c][h][:], ACT.Abs)
+            for t in range(PACK):
+                nc.vector.tensor_scalar_add(y[:, t, :], dist[:, t, :], bias[:, t : t + 1])
+            nc.sync.dma_start(y_rows[:, :, cols], y[:])
+            interleave(nc.vector.tensor_copy, y_grouped[:], y[:])
+            quantize(y_codes[:, cols], y_scales[:, cols], y_grouped[:])
+            nc.sync.dma_start(y_words[:, cols], y_codes[:, cols].bitcast(I32))
+
+        for c in range(CHUNKS):
+            gather(z_picked, z_plane, z_list, z_wgt, 3, c * CHUNK, (c + 1) * CHUNK)
+        front(0)
+        front(1)
+        back(0)
+        front(2)
+        back(1)
+        front(3)
+        back(2)
+        back(3)
+        for q in range(4):
+            eng = nc.sync if q % 2 == 0 else nc.scalar
+            eng.dma_start(
+                out_2[0, 4 * q : 4 * q + 4, :].bitcast(I32), y_scales[32 * q : 32 * q + 4, :].bitcast(I32)
+            )

@@ -1,6 +1,7 @@
 from contextlib import ExitStack
 
 import concourse.mybir as mybir
+from concourse.masks import make_identity
 
 K, L, N, T, J = 512, 512, 512, 2048, 1024
 FLOPS = 2 * (K + L) * N * J
@@ -48,8 +49,8 @@ def tile_list_absd_biasP_kernel(
         z_rows = zT.rearrange("(p i) t -> p i t", i=PACK)
         x_list = keep.tile([P, J // LANES], U16, name="x_list")
         z_list = keep.tile([P, J // LANES], U16, name="z_list")
-        x_plane = [keep.tile([P, T], F32, name="x_plane%d" % i) for i in range(PACK)]
-        z_plane = [keep.tile([P, T], F32, name="z_plane%d" % i) for i in range(PACK)]
+        x_plane = [keep.tile([P, T], F32, name="x_plane%d" % i, tag="x_plane%d" % i, align_bytes=64) for i in range(PACK)]
+        z_plane = [keep.tile([P, T], F32, name="z_plane%d" % i, tag="z_plane%d" % i, align_bytes=64) for i in range(PACK)]
         x_wgt = keep.tile([P, J], F32, name="x_wgt")
         z_wgt = keep.tile([P, J], F32, name="z_wgt")
         wa_raw = keep.tile([P, PACK, N], F32, name="wa_raw")
@@ -57,26 +58,48 @@ def tile_list_absd_biasP_kernel(
         wb_scale_raw = keep.tile([P, N], U8, name="wb_scale_raw")
         bias = keep.tile([P, PACK], F32, name="bias")
 
+        wgt_rows = keep.tile([P, HALF], F32, name="wgt_rows")
+        identity = keep.tile([P, P], F32, name="identity")
+        nc.gpsimd.memset(wb_scale_raw[:].bitcast(I32), 0)
+        nc.vector.memset(wgt_rows[32:64, :], 0.0)
+        nc.vector.memset(wgt_rows[64:P, :], 0.0)
+        make_identity(nc, identity[:])
+        nc.sync.dma_start(wgt_rows[0:16, :], wgt.rearrange("p (h j) -> (p h) j", h=2)[0 : 2 * P : 17, :])
+        nc.sync.dma_start(wgt_rows[16:32, :], wgt2.rearrange("p (h j) -> (p h) j", h=2)[0 : 2 * P : 17, :])
+        nc.sync.dma_start(wb_raw[:].bitcast(I32), wb_words[0].bitcast(I32))
         nc.sync.dma_start(x_list[:], offs)
         nc.sync.dma_start(x_plane[0][:], x_rows[:, 0, :])
-        nc.sync.dma_start(x_wgt[:, :HALF], wgt[:, :HALF])
-        nc.sync.dma_start(x_wgt[:, HALF:], wgt[:, HALF:])
-        nc.sync.dma_start(wb_raw[:].bitcast(I32), wb_words[0].bitcast(I32))
-        nc.gpsimd.memset(wb_scale_raw[:].bitcast(I32), 0)
         for q in range(4):
-            nc.gpsimd.dma_start(
+            nc.sync.dma_start(
                 wb_scale_raw[32 * q : 32 * q + 4, :].bitcast(I32), wb_scales[0, 4 * q : 4 * q + 4, :].bitcast(I32)
             )
-        nc.gpsimd.dma_start(bias[:], b.rearrange("(p t) -> p t", t=PACK))
         for i in range(1, PACK):
             nc.sync.dma_start(x_plane[i][:], x_rows[:, i, :])
         nc.sync.dma_start(z_list[:], offs2)
-        nc.sync.dma_start(z_wgt[:], wgt2)
+        nc.sync.dma_start(bias[:], b.rearrange("(p t) -> p t", t=PACK))
         nc.sync.dma_start(z_plane[0][:], z_rows[:, 0, :])
         nc.sync.dma_start(z_plane[1][:], z_rows[:, 1, :])
         nc.sync.dma_start(wa_raw[:], wa.rearrange("(p i) n -> p i n", i=PACK))
         nc.sync.dma_start(z_plane[2][:], z_rows[:, 2, :])
         nc.sync.dma_start(z_plane[3][:], z_rows[:, 3, :])
+
+        turned = psum.tile([P, PACK, P], F32, name="turned", tag="bank0")
+        for c in range(PACK):
+            nc.tensor.transpose(turned[:, c, :], wgt_rows[:, c * P : (c + 1) * P], identity[:])
+        for w, spread in enumerate((x_wgt, z_wgt)):
+            for h in range(2):
+                repeated = keep.tile([P, PACK, 8, LANES], F32, name="repeated%d_%d" % (w, h))
+                first = 16 * w + h
+                nc.scalar.copy(
+                    repeated[:],
+                    turned[:, :, first : first + 15 : 2].unsqueeze(3).to_broadcast([P, PACK, 8, LANES]),
+                )
+                back_turned = psum.tile([P, PACK, P], F32, name="back_turned%d_%d" % (w, h), tag="bank%d" % (1 + 2 * w + h))
+                for c in range(PACK):
+                    nc.tensor.transpose(
+                        back_turned[:, c, :], repeated[:, c, :, :].rearrange("p g r -> p (g r)"), identity[:]
+                    )
+                nc.scalar.copy(spread[:, h * HALF : (h + 1) * HALF], back_turned[:].rearrange("p c i -> p (c i)"))
 
         def gather(picked, plane, lists, weights, i, j0, j1):
             nc.vector.tensor_tensor(
@@ -89,36 +112,35 @@ def tile_list_absd_biasP_kernel(
         x_picked = keep.tile([P, PACK, J], F32, name="x_picked")
         z_picked = keep.tile([P, PACK, J], F32, name="z_picked")
         x_grouped = keep.tile([P, J, PACK], BF16, name="x_grouped", align_bytes=64)
-        z_grouped = keep.tile([P, J, PACK], BF16, name="z_grouped", align_bytes=64)
-        x_codes = keep.tile([P, J], U32, name="x_codes", align_bytes=64)
         z_codes = keep.tile([P, J], U32, name="z_codes", align_bytes=64)
         x_scales = keep.tile([P, J], U8, name="x_scales", align_bytes=64)
         z_scales = keep.tile([P, J], U8, name="z_scales", align_bytes=64)
+
+        wb_codes = keep.tile([P, PACK, 2 * P], U8, name="wb_codes", align_bytes=64)
+        nc.vector.tensor_copy(
+            wb_codes[:].rearrange("p t (m e) -> p t m e", e=2),
+            wb_raw[:].rearrange("p (m t e) -> p t m e", t=PACK, e=2),
+        )
 
         gather(x_picked, x_plane, x_list, x_wgt, 0, 0, HALF)
         gather(x_picked, x_plane, x_list, x_wgt, 0, HALF, J)
         gather(x_picked, x_plane, x_list, x_wgt, 1, 0, J)
 
-        wb_codes = keep.tile([P, PACK, 2 * P], U8, name="wb_codes", align_bytes=64)
-        wb_scale = keep.tile([P, PACK, P], U8, name="wb_scale", align_bytes=64)
-        nc.vector.tensor_copy(
-            wb_codes[:].rearrange("p t (m e) -> p t m e", e=2),
-            wb_raw[:].rearrange("p (m t e) -> p t m e", t=PACK, e=2),
-        )
+        wb_scale = keep.tile([P, PACK, P], U8, name="wb_scale", tag="x_plane1", align_bytes=64)
         nc.vector.tensor_copy(wb_scale[:], wb_scale_raw[:].rearrange("p (m t) -> p t m", t=PACK))
-
         gather(x_picked, x_plane, x_list, x_wgt, 2, 0, J)
         gather(x_picked, x_plane, x_list, x_wgt, 3, 0, HALF)
         gather(x_picked, x_plane, x_list, x_wgt, 3, HALF, J)
         for j0 in (0, HALF):
             interleave(nc.scalar.copy, x_grouped[:, j0 : j0 + HALF, :], x_picked[:, :, j0 : j0 + HALF])
-        gather(z_picked, z_plane, z_list, z_wgt, 0, 0, J)
-        gather(z_picked, z_plane, z_list, z_wgt, 1, 0, J)
-        for j0 in (0, HALF):
-            quantize(x_codes[:, j0 : j0 + HALF], x_scales[:, j0 : j0 + HALF], x_grouped[:, j0 : j0 + HALF, :])
+        x_codes = []
+        for h in range(2):
+            gather(z_picked, z_plane, z_list, z_wgt, h, 0, J)
+            cols = slice(h * HALF, (h + 1) * HALF)
+            x_codes.append(keep.tile([P, HALF], U32, name="x_codes%d" % h, tag="z_plane%d" % h, align_bytes=64))
+            quantize(x_codes[h][:], x_scales[:, cols], x_grouped[:, cols, :])
 
         wa_grouped = keep.tile([P, N, PACK], BF16, name="wa_grouped", align_bytes=64)
-        wa_codes = keep.tile([P, N], U32, name="wa_codes", align_bytes=64)
         wa_scales = keep.tile([P, N], U8, name="wa_scales", align_bytes=64)
         nc.scalar.activation(
             wa_grouped[:].rearrange("p (t m) i -> p m i t", t=PACK),
@@ -127,9 +149,10 @@ def tile_list_absd_biasP_kernel(
             scale=-1.0,
         )
         gather(z_picked, z_plane, z_list, z_wgt, 2, 0, J)
+        wa_codes = keep.tile([P, N], U32, name="wa_codes", tag="z_plane2", align_bytes=64)
         quantize(wa_codes[:], wa_scales[:], wa_grouped[:])
 
-        banks = [[psum.tile([P, 2, CHUNK], F32, name="bank%d_%d" % (c, h)) for h in range(2)] for c in range(CHUNKS)]
+        banks = [[psum.tile([P, 2, CHUNK], F32, name="sums%d_%d" % (c, h), tag="bank%d" % (2 * c + h)) for h in range(2)] for c in range(CHUNKS)]
         for c in range(CHUNKS):
             cols = slice(c * CHUNK, (c + 1) * CHUNK)
             for t in range(PACK):
@@ -137,7 +160,7 @@ def tile_list_absd_biasP_kernel(
                     out=banks[c][t // 2][:, t % 2, :],
                     lhsT=wa_codes[:, t * P : (t + 1) * P].bitcast(FP8X4),
                     lhsT_scale=wa_scales[:, t * P : (t + 1) * P],
-                    rhs=x_codes[:, cols].bitcast(FP8X4),
+                    rhs=x_codes[c // 2][:, (c % 2) * CHUNK : (c % 2 + 1) * CHUNK].bitcast(FP8X4),
                     rhs_scale=x_scales[:, cols],
                     start=(t % 2 == 0),
                     stop=False,
@@ -150,8 +173,9 @@ def tile_list_absd_biasP_kernel(
 
         def front(c):
             cols = slice(c * CHUNK, (c + 1) * CHUNK)
-            interleave(nc.scalar.copy, z_grouped[:, cols, :], z_picked[:, :, cols])
-            quantize(z_codes[:, cols], z_scales[:, cols], z_grouped[:, cols, :])
+            z_grouped = keep.tile([P, CHUNK, PACK], BF16, name="z_grouped", bufs=2, align_bytes=64)
+            interleave(nc.scalar.copy if c < 2 else nc.vector.tensor_copy, z_grouped[:], z_picked[:, :, cols])
+            quantize(z_codes[:, cols], z_scales[:, cols], z_grouped[:])
             for t in range(PACK):
                 for s in range(CHUNK // FP4_N):
                     part = slice(c * CHUNK + s * FP4_N, c * CHUNK + (s + 1) * FP4_N)
@@ -175,7 +199,7 @@ def tile_list_absd_biasP_kernel(
             for t in range(PACK):
                 nc.vector.tensor_scalar_add(y[:, t, :], dist[:, t, :], bias[:, t : t + 1])
             nc.sync.dma_start(y_rows[:, :, cols], y[:])
-            interleave(nc.vector.tensor_copy, y_grouped[:], y[:])
+            interleave(nc.scalar.copy if c in (1, 2) else nc.vector.tensor_copy, y_grouped[:], y[:])
             quantize(y_codes[:, cols], y_scales[:, cols], y_grouped[:])
             nc.sync.dma_start(y_words[:, cols], y_codes[:, cols].bitcast(I32))
 

@@ -143,8 +143,8 @@ def tile_list_absd_biasP_kernel(
         wa_grouped = keep.tile([P, N, PACK], BF16, name="wa_grouped", align_bytes=64)
         wa_scales = keep.tile([P, N], U8, name="wa_scales", align_bytes=64)
         nc.scalar.activation(
-            wa_grouped[:].rearrange("p (t m) i -> p m i t", t=PACK),
-            wa_raw[:].rearrange("p i (m t) -> p m i t", t=PACK),
+            wa_grouped[:].rearrange("p (t m) i -> p m t i", t=PACK),
+            wa_raw[:].rearrange("p i (m t) -> p m t i", t=PACK),
             ACT.Copy,
             scale=-1.0,
         )

@@ -51,8 +51,8 @@ def tile_list_absd_biasP_kernel(
         z_list = keep.tile([P, J // LANES], U16, name="z_list")
         x_plane = [keep.tile([P, T], F32, name="x_plane%d" % i, tag="x_plane%d" % i, align_bytes=64) for i in range(PACK)]
         z_plane = [keep.tile([P, T], F32, name="z_plane%d" % i, tag="z_plane%d" % i, align_bytes=64) for i in range(PACK)]
-        x_wgt = keep.tile([P, J], F32, name="x_wgt")
-        z_wgt = keep.tile([P, J], F32, name="z_wgt")
+        x_wgt = [keep.tile([P, HALF], F32, name="x_wgt%d" % h) for h in range(2)]
+        z_wgt = [keep.tile([P, HALF], F32, name="z_wgt%d" % h) for h in range(2)]
         wa_raw = keep.tile([P, PACK, N], F32, name="wa_raw")
         wb_raw = keep.tile([P, 2 * N], U8, name="wb_raw")
         wb_scale_raw = keep.tile([P, N], U8, name="wb_scale_raw")
@@ -78,40 +78,50 @@ def tile_list_absd_biasP_kernel(
         nc.sync.dma_start(z_list[:], offs2)
         nc.sync.dma_start(bias[:], b.rearrange("(p t) -> p t", t=PACK))
         nc.sync.dma_start(z_plane[0][:], z_rows[:, 0, :])
-        nc.sync.dma_start(z_plane[1][:], z_rows[:, 1, :])
         nc.sync.dma_start(wa_raw[:], wa.rearrange("(p i) n -> p i n", i=PACK))
+        nc.sync.dma_start(z_plane[1][:], z_rows[:, 1, :])
         nc.sync.dma_start(z_plane[2][:], z_rows[:, 2, :])
         nc.sync.dma_start(z_plane[3][:], z_rows[:, 3, :])
 
-        turned = psum.tile([P, PACK, P], F32, name="turned", tag="bank0")
-        for c in range(PACK):
-            nc.tensor.transpose(turned[:, c, :], wgt_rows[:, c * P : (c + 1) * P], identity[:])
+        turned = []
+        for u in range(2):
+            turned.append(psum.tile([P, 2, P], F32, name="turned%d" % u, tag="bank%d" % u))
+            for c in range(2):
+                block = slice((2 * u + c) * P, (2 * u + c + 1) * P)
+                nc.tensor.transpose(turned[u][:, c, :], wgt_rows[:, block], identity[:])
         for w, spread in enumerate((x_wgt, z_wgt)):
             for h in range(2):
-                repeated = keep.tile([P, PACK, 8, LANES], F32, name="repeated%d_%d" % (w, h))
-                first = 16 * w + h
-                nc.scalar.copy(
-                    repeated[:],
-                    turned[:, :, first : first + 15 : 2].unsqueeze(3).to_broadcast([P, PACK, 8, LANES]),
-                )
-                back_turned = psum.tile([P, PACK, P], F32, name="back_turned%d_%d" % (w, h), tag="bank%d" % (1 + 2 * w + h))
-                for c in range(PACK):
-                    nc.tensor.transpose(
-                        back_turned[:, c, :], repeated[:, c, :, :].rearrange("p g r -> p (g r)"), identity[:]
+                for u in range(2):
+                    repeated = keep.tile([P, 2, 8, LANES], F32, name="repeated", bufs=4)
+                    first = 16 * w + h
+                    nc.scalar.copy(
+                        repeated[:],
+                        turned[u][:, :, first : first + 15 : 2].unsqueeze(3).to_broadcast([P, 2, 8, LANES]),
                     )
-                nc.scalar.copy(spread[:, h * HALF : (h + 1) * HALF], back_turned[:].rearrange("p c i -> p (c i)"))
+                    back_turned = psum.tile([P, 2, P], F32, name="back_turned", tag="bank%d" % (2 + 2 * h + u))
+                    for c in range(2):
+                        nc.tensor.transpose(
+                            back_turned[:, c, :], repeated[:, c, :, :].rearrange("p g r -> p (g r)"), identity[:]
+                        )
+                    nc.scalar.copy(
+                        spread[h][:, u * CHUNK : (u + 1) * CHUNK], back_turned[:].rearrange("p c i -> p (c i)")
+                    )
 
-        def gather(picked, plane, lists, weights, i, j0, j1):
+        def gather(picked, plane, lists, weights, j0, width):
+            h, start = divmod(j0, HALF)
             nc.vector.tensor_tensor(
-                picked[:, i, j0:j1],
-                plane[i][:].indirect(lists[:, j0 // LANES : j1 // LANES]),
-                weights[:, j0:j1],
+                picked,
+                plane[:].indirect(lists[:, j0 // LANES : (j0 + width) // LANES]),
+                weights[h][:, start : start + width],
                 MULT,
             )
 
-        x_picked = keep.tile([P, PACK, J], F32, name="x_picked")
-        z_picked = keep.tile([P, PACK, J], F32, name="z_picked")
-        x_grouped = keep.tile([P, J, PACK], BF16, name="x_grouped", align_bytes=64)
+        x_picked = [keep.tile([P, PACK, HALF], F32, name="x_picked%d" % h) for h in range(2)]
+        z_early = [keep.tile([P, 2, HALF], F32, name="z_early%d" % h) for h in range(2)]
+        z_grouped = [
+            keep.tile([P, CHUNK, PACK], BF16, name="z_grouped%d" % c, tag="z_grouped%d" % c, align_bytes=64)
+            for c in range(CHUNKS)
+        ]
         z_codes = keep.tile([P, J], U32, name="z_codes", align_bytes=64)
         x_scales = keep.tile([P, J], U8, name="x_scales", align_bytes=64)
         z_scales = keep.tile([P, J], U8, name="z_scales", align_bytes=64)
@@ -121,25 +131,18 @@ def tile_list_absd_biasP_kernel(
             wb_codes[:].rearrange("p t (m e) -> p t m e", e=2),
             wb_raw[:].rearrange("p (m t e) -> p t m e", t=PACK, e=2),
         )
-
-        gather(x_picked, x_plane, x_list, x_wgt, 0, 0, HALF)
-        gather(x_picked, x_plane, x_list, x_wgt, 0, HALF, J)
-        gather(x_picked, x_plane, x_list, x_wgt, 1, 0, J)
-
-        wb_scale = keep.tile([P, PACK, P], U8, name="wb_scale", tag="x_plane1", align_bytes=64)
-        nc.vector.tensor_copy(wb_scale[:], wb_scale_raw[:].rearrange("p (m t) -> p t m", t=PACK))
-        gather(x_picked, x_plane, x_list, x_wgt, 2, 0, J)
-        gather(x_picked, x_plane, x_list, x_wgt, 3, 0, HALF)
-        gather(x_picked, x_plane, x_list, x_wgt, 3, HALF, J)
-        for j0 in (0, HALF):
-            interleave(nc.scalar.copy, x_grouped[:, j0 : j0 + HALF, :], x_picked[:, :, j0 : j0 + HALF])
-        x_codes = []
+        for i in range(PACK):
+            width = CHUNK if i == 0 else HALF
+            for j0 in range(0, J, width):
+                h, start = divmod(j0, HALF)
+                gather(x_picked[h][:, i, start : start + width], x_plane[i], x_list, x_wgt, j0, width)
+            if i == 1:
+                wb_scale = keep.tile([P, PACK, P], U8, name="wb_scale", tag="x_plane1", align_bytes=64)
+                nc.vector.tensor_copy(wb_scale[:], wb_scale_raw[:].rearrange("p (m t) -> p t m", t=PACK))
+        x_grouped = []
         for h in range(2):
-            gather(z_picked, z_plane, z_list, z_wgt, h, 0, J)
-            cols = slice(h * HALF, (h + 1) * HALF)
-            x_codes.append(keep.tile([P, HALF], U32, name="x_codes%d" % h, tag="z_plane%d" % h, align_bytes=64))
-            quantize(x_codes[h][:], x_scales[:, cols], x_grouped[:, cols, :])
-
+            x_grouped.append(keep.tile([P, HALF, PACK], BF16, name="x_grouped%d" % h, tag="x_grouped%d" % h, align_bytes=64))
+            interleave(nc.scalar.copy, x_grouped[h][:], x_picked[h][:])
         wa_grouped = keep.tile([P, N, PACK], BF16, name="wa_grouped", align_bytes=64)
         wa_scales = keep.tile([P, N], U8, name="wa_scales", align_bytes=64)
         nc.scalar.activation(
@@ -148,9 +151,17 @@ def tile_list_absd_biasP_kernel(
             ACT.Copy,
             scale=-1.0,
         )
-        gather(z_picked, z_plane, z_list, z_wgt, 2, 0, J)
-        wa_codes = keep.tile([P, N], U32, name="wa_codes", tag="z_plane2", align_bytes=64)
+        x_codes = []
+        for i in range(2):
+            for h in range(2):
+                gather(z_early[h][:, i, :], z_plane[i], z_list, z_wgt, h * HALF, HALF)
+            x_codes.append(keep.tile([P, HALF], U32, name="x_codes%d" % i, tag="z_plane%d" % i, align_bytes=64))
+            quantize(x_codes[i][:], x_scales[:, i * HALF : (i + 1) * HALF], x_grouped[i][:])
+        wa_codes = keep.tile([P, N], U32, name="wa_codes", tag="x_grouped1", align_bytes=64)
         quantize(wa_codes[:], wa_scales[:], wa_grouped[:])
+        for c in range(CHUNKS):
+            local = slice((c % 2) * CHUNK, (c % 2 + 1) * CHUNK)
+            interleave(nc.scalar.copy, z_grouped[c][:, :, 0:2], z_early[c // 2][:, :, local])
 
         banks = [[psum.tile([P, 2, CHUNK], F32, name="sums%d_%d" % (c, h), tag="bank%d" % (2 * c + h)) for h in range(2)] for c in range(CHUNKS)]
         for c in range(CHUNKS):
@@ -173,9 +184,8 @@ def tile_list_absd_biasP_kernel(
 
         def front(c):
             cols = slice(c * CHUNK, (c + 1) * CHUNK)
-            z_grouped = keep.tile([P, CHUNK, PACK], BF16, name="z_grouped", bufs=2, align_bytes=64)
-            interleave(nc.scalar.copy if c < 2 else nc.vector.tensor_copy, z_grouped[:], z_picked[:, :, cols])
-            quantize(z_codes[:, cols], z_scales[:, cols], z_grouped[:])
+            interleave(nc.scalar.copy, z_grouped[c][:, :, 2:PACK], z_late[c][:])
+            quantize(z_codes[:, cols], z_scales[:, cols], z_grouped[c][:])
             for t in range(PACK):
                 for s in range(CHUNK // FP4_N):
                     part = slice(c * CHUNK + s * FP4_N, c * CHUNK + (s + 1) * FP4_N)
@@ -189,30 +199,47 @@ def tile_list_absd_biasP_kernel(
                         stop=(t % 2 == 1 and s == CHUNK // FP4_N - 1),
                     )
 
-        def back(c):
-            cols = slice(c * CHUNK, (c + 1) * CHUNK)
-            dist = keep.tile([P, PACK, CHUNK], F32, name="dist%d" % c)
-            y = keep.tile([P, PACK, CHUNK], F32, name="y%d" % c)
-            y_grouped = keep.tile([P, CHUNK, PACK], BF16, name="y_grouped%d" % c, align_bytes=64)
+        dist = [keep.tile([P, PACK, CHUNK], F32, name="dist%d" % c) for c in range(CHUNKS)]
+        y = [keep.tile([P, PACK, CHUNK], F32, name="y%d" % c) for c in range(CHUNKS)]
+
+        def distance(c):
             for h in range(2):
-                nc.scalar.activation(dist[:, 2 * h : 2 * h + 2, :], banks[c][h][:], ACT.Abs)
+                nc.scalar.activation(dist[c][:, 2 * h : 2 * h + 2, :], banks[c][h][:], ACT.Abs)
+
+        def add_bias(c):
             for t in range(PACK):
-                nc.vector.tensor_scalar_add(y[:, t, :], dist[:, t, :], bias[:, t : t + 1])
-            nc.sync.dma_start(y_rows[:, :, cols], y[:])
-            interleave(nc.scalar.copy if c in (1, 2) else nc.vector.tensor_copy, y_grouped[:], y[:])
+                nc.vector.tensor_scalar_add(y[c][:, t, :], dist[c][:, t, :], bias[:, t : t + 1])
+            nc.sync.dma_start(y_rows[:, :, c * CHUNK : (c + 1) * CHUNK], y[c][:])
+
+        def hand_on(c):
+            cols = slice(c * CHUNK, (c + 1) * CHUNK)
+            y_grouped = keep.tile([P, CHUNK, PACK], BF16, name="y_grouped%d" % c, align_bytes=64)
+            interleave(nc.scalar.copy if c < 2 else nc.vector.tensor_copy, y_grouped[:], y[c][:])
             quantize(y_codes[:, cols], y_scales[:, cols], y_grouped[:])
             nc.sync.dma_start(y_words[:, cols], y_codes[:, cols].bitcast(I32))
 
-        for c in range(CHUNKS):
-            gather(z_picked, z_plane, z_list, z_wgt, 3, c * CHUNK, (c + 1) * CHUNK)
+        z_late = []
+
+        def late_gathers(c, planes):
+            if len(z_late) == c:
+                tag = "z_late%d" % c if c < 2 else "z_grouped%d" % (c - 2)
+                z_late.append(keep.tile([P, 2, CHUNK], F32, name="z_late%d" % c, tag=tag, align_bytes=64))
+            for i in planes:
+                gather(z_late[c][:, i - 2, :], z_plane[i], z_list, z_wgt, c * CHUNK, CHUNK)
+
+        for i in (2, 3):
+            for c in range(2):
+                late_gathers(c, [i])
         front(0)
         front(1)
-        back(0)
-        front(2)
-        back(1)
-        front(3)
-        back(2)
-        back(3)
+        for c in range(CHUNKS):
+            distance(c)
+            add_bias(c)
+            if c + 2 < CHUNKS:
+                late_gathers(c + 2, [2, 3])
+                front(c + 2)
+        for c in range(CHUNKS):
+            hand_on(c)
         for q in range(4):
             eng = nc.sync if q % 2 == 0 else nc.scalar
             eng.dma_start(

@@ -14,16 +14,21 @@ U16 = mybir.dt.uint16
 U8 = mybir.dt.uint8
 FP8X4 = mybir.dt.float8_e4m3fn_x4
 FP4X4 = mybir.dt.float4_e2m1fn_x4
-MULT = mybir.AluOpType.mult
 ACT = mybir.ActivationFunctionType
 
 P = 128
 PACK = 4
-LANES = 16
+HEADS = 8
+LANES = P // HEADS
+QUADRANT = 32
+SCALE_ROWS = 4
+HALF = J // 2
 CHUNK = 256
 CHUNKS = J // CHUNK
-HALF = J // 2
 FP4_N = 128
+MX_ALIGN = 64
+AHEAD = 3
+SCALAR_ROUNDS = 2
 
 
 def tile_list_absd_biasP_kernel(
@@ -34,44 +39,56 @@ def tile_list_absd_biasP_kernel(
         keep = ctx.enter_context(tc.tile_pool(name="keep", bufs=1))
         psum = ctx.enter_context(tc.psum_pool(name="psum", bufs=1))
 
-        def interleave(copy, grouped, planes):
+        def group(copy, grouped, planes):
             copy(
-                grouped.rearrange("p (c i) t -> p c t i", i=PACK),
-                planes.rearrange("p t (c i) -> p c t i", i=PACK),
+                grouped.rearrange("p (c e) i -> p c i e", e=4),
+                planes.rearrange("p i (c e) -> p c i e", e=4),
             )
 
         def quantize(codes, scales, grouped):
-            nc.vector.quantize_mx(
-                out=codes.bitcast(FP8X4), scales=scales, in_=grouped.rearrange("p j t -> p (j t)")
+            nc.vector.quantize_mx(out=codes.bitcast(FP8X4), scales=scales, in_=grouped.rearrange("p j i -> p (j i)"))
+
+        def gather(picked, plane, lists, weights, j0, width):
+            nc.vector.tensor_tensor(
+                picked,
+                plane[:].indirect(lists[:, j0 // LANES : (j0 + width) // LANES]),
+                weights[:, j0 : j0 + width],
+                mybir.AluOpType.mult,
             )
 
-        x_rows = xT.rearrange("(p i) t -> p i t", i=PACK)
-        z_rows = zT.rearrange("(p i) t -> p i t", i=PACK)
+        def chunk(c):
+            return slice(c * CHUNK, (c + 1) * CHUNK)
+
+        x_plane = [keep.tile([P, T], F32, name="x_plane%d" % i, tag="x_plane%d" % i, align_bytes=MX_ALIGN) for i in range(PACK)]
+        z_plane = [keep.tile([P, T], F32, name="z_plane%d" % i, tag="z_plane%d" % i, align_bytes=MX_ALIGN) for i in range(PACK)]
         x_list = keep.tile([P, J // LANES], U16, name="x_list")
         z_list = keep.tile([P, J // LANES], U16, name="z_list")
-        x_plane = [keep.tile([P, T], F32, name="x_plane%d" % i, tag="x_plane%d" % i, align_bytes=64) for i in range(PACK)]
-        z_plane = [keep.tile([P, T], F32, name="z_plane%d" % i, tag="z_plane%d" % i, align_bytes=64) for i in range(PACK)]
-        x_wgt = [keep.tile([P, HALF], F32, name="x_wgt%d" % h) for h in range(2)]
-        z_wgt = [keep.tile([P, HALF], F32, name="z_wgt%d" % h) for h in range(2)]
+        wgt_rows = keep.tile([P, HALF], F32, name="wgt_rows")
         wa_raw = keep.tile([P, PACK, N], F32, name="wa_raw")
         wb_raw = keep.tile([P, 2 * N], U8, name="wb_raw")
         wb_scale_raw = keep.tile([P, N], U8, name="wb_scale_raw")
         bias = keep.tile([P, PACK], F32, name="bias")
-
-        wgt_rows = keep.tile([P, HALF], F32, name="wgt_rows")
         identity = keep.tile([P, P], F32, name="identity")
+
         nc.gpsimd.memset(wb_scale_raw[:].bitcast(I32), 0)
-        nc.vector.memset(wgt_rows[32:64, :], 0.0)
-        nc.vector.memset(wgt_rows[64:P, :], 0.0)
+        nc.vector.memset(wgt_rows[QUADRANT : 2 * QUADRANT, :], 0.0)
+        nc.vector.memset(wgt_rows[2 * QUADRANT :, :], 0.0)
         make_identity(nc, identity[:])
-        nc.sync.dma_start(wgt_rows[0:16, :], wgt.rearrange("p (h j) -> (p h) j", h=2)[0 : 2 * P : 17, :])
-        nc.sync.dma_start(wgt_rows[16:32, :], wgt2.rearrange("p (h j) -> (p h) j", h=2)[0 : 2 * P : 17, :])
-        nc.sync.dma_start(wb_raw[:].bitcast(I32), wb_words[0].bitcast(I32))
+
+        x_rows = xT.rearrange("(p i) t -> p i t", i=PACK)
+        z_rows = zT.rearrange("(p i) t -> p i t", i=PACK)
+        step = LANES + 1
+        nc.sync.dma_start(wgt_rows[: 2 * HEADS, :], wgt.rearrange("p (h j) -> (p h) j", h=2)[0 : 2 * P : step, :])
+        nc.scalar.dma_start(
+            wgt_rows[2 * HEADS : 4 * HEADS, :], wgt2.rearrange("p (h j) -> (p h) j", h=2)[0 : 2 * P : step, :]
+        )
+        nc.scalar.dma_start(wb_raw[:].bitcast(I32), wb_words[0].bitcast(I32))
         nc.sync.dma_start(x_list[:], offs)
         nc.sync.dma_start(x_plane[0][:], x_rows[:, 0, :])
-        for q in range(4):
+        for q in range(P // QUADRANT):
             nc.sync.dma_start(
-                wb_scale_raw[32 * q : 32 * q + 4, :].bitcast(I32), wb_scales[0, 4 * q : 4 * q + 4, :].bitcast(I32)
+                wb_scale_raw[QUADRANT * q : QUADRANT * q + SCALE_ROWS, :].bitcast(I32),
+                wb_scales[0, SCALE_ROWS * q : SCALE_ROWS * (q + 1), :].bitcast(I32),
             )
         for i in range(1, PACK):
             nc.sync.dma_start(x_plane[i][:], x_rows[:, i, :])
@@ -79,118 +96,110 @@ def tile_list_absd_biasP_kernel(
         nc.sync.dma_start(bias[:], b.rearrange("(p t) -> p t", t=PACK))
         nc.sync.dma_start(z_plane[0][:], z_rows[:, 0, :])
         nc.sync.dma_start(wa_raw[:], wa.rearrange("(p i) n -> p i n", i=PACK))
-        nc.sync.dma_start(z_plane[1][:], z_rows[:, 1, :])
-        nc.sync.dma_start(z_plane[2][:], z_rows[:, 2, :])
-        nc.sync.dma_start(z_plane[3][:], z_rows[:, 3, :])
+        for i in range(1, PACK):
+            nc.sync.dma_start(z_plane[i][:], z_rows[:, i, :])
 
+        x_wgt = keep.tile([P, J], F32, name="x_wgt")
+        z_wgt = keep.tile([P, J], F32, name="z_wgt")
+        blocks = CHUNK // P
         turned = []
-        for u in range(2):
-            turned.append(psum.tile([P, 2, P], F32, name="turned%d" % u, tag="bank%d" % u))
-            for c in range(2):
-                block = slice((2 * u + c) * P, (2 * u + c + 1) * P)
-                nc.tensor.transpose(turned[u][:, c, :], wgt_rows[:, block], identity[:])
-        for w, spread in enumerate((x_wgt, z_wgt)):
-            for h in range(2):
-                for u in range(2):
-                    repeated = keep.tile([P, 2, 8, LANES], F32, name="repeated", bufs=4)
-                    first = 16 * w + h
-                    nc.scalar.copy(
-                        repeated[:],
-                        turned[u][:, :, first : first + 15 : 2].unsqueeze(3).to_broadcast([P, 2, 8, LANES]),
-                    )
-                    back_turned = psum.tile([P, 2, P], F32, name="back_turned", tag="bank%d" % (2 + 2 * h + u))
-                    for c in range(2):
-                        nc.tensor.transpose(
-                            back_turned[:, c, :], repeated[:, c, :, :].rearrange("p g r -> p (g r)"), identity[:]
-                        )
-                    nc.scalar.copy(
-                        spread[h][:, u * CHUNK : (u + 1) * CHUNK], back_turned[:].rearrange("p c i -> p (c i)")
-                    )
+        for u in range(HALF // CHUNK):
+            turned.append(psum.tile([P, blocks, P], F32, name="turned%d" % u, tag="bank%d" % u))
+            for s in range(blocks):
+                first = u * CHUNK + s * P
+                nc.tensor.transpose(turned[u][:, s, :], wgt_rows[:, first : first + P], identity[:])
+        for w, weights in enumerate((x_wgt, z_wgt)):
+            for c in range(CHUNKS):
+                h, u = divmod(c, HALF // CHUNK)
+                heads = turned[u][:, :, 2 * HEADS * w + h : 2 * HEADS * (w + 1) + h - 1 : 2]
+                repeated = keep.tile([P, blocks, HEADS, LANES], F32, name="repeated", bufs=CHUNKS)
+                nc.scalar.copy(repeated[:], heads.unsqueeze(3).to_broadcast([P, blocks, HEADS, LANES]))
+                spread = psum.tile([P, blocks, P], F32, name="spread", tag="bank%d" % (len(turned) + c))
+                for s in range(blocks):
+                    nc.tensor.transpose(spread[:, s, :], repeated[:, s, :, :].rearrange("p g r -> p (g r)"), identity[:])
+                nc.scalar.copy(weights[:, chunk(c)], spread[:].rearrange("p s j -> p (s j)"))
 
-        def gather(picked, plane, lists, weights, j0, width):
-            h, start = divmod(j0, HALF)
-            nc.vector.tensor_tensor(
-                picked,
-                plane[:].indirect(lists[:, j0 // LANES : (j0 + width) // LANES]),
-                weights[h][:, start : start + width],
-                MULT,
-            )
-
-        x_picked = [keep.tile([P, PACK, HALF], F32, name="x_picked%d" % h) for h in range(2)]
-        z_early = [keep.tile([P, 2, HALF], F32, name="z_early%d" % h) for h in range(2)]
-        z_grouped = [
-            keep.tile([P, CHUNK, PACK], BF16, name="z_grouped%d" % c, tag="z_grouped%d" % c, align_bytes=64)
-            for c in range(CHUNKS)
-        ]
-        z_codes = keep.tile([P, J], U32, name="z_codes", align_bytes=64)
-        x_scales = keep.tile([P, J], U8, name="x_scales", align_bytes=64)
-        z_scales = keep.tile([P, J], U8, name="z_scales", align_bytes=64)
-
-        wb_codes = keep.tile([P, PACK, 2 * P], U8, name="wb_codes", align_bytes=64)
+        wb_codes = keep.tile([P, PACK, 2 * P], U8, name="wb_codes", align_bytes=MX_ALIGN)
         nc.vector.tensor_copy(
             wb_codes[:].rearrange("p t (m e) -> p t m e", e=2),
             wb_raw[:].rearrange("p (m t e) -> p t m e", t=PACK, e=2),
         )
-        for i in range(PACK):
-            width = CHUNK if i == 0 else HALF
-            for j0 in range(0, J, width):
-                h, start = divmod(j0, HALF)
-                gather(x_picked[h][:, i, start : start + width], x_plane[i], x_list, x_wgt, j0, width)
-            if i == 1:
-                wb_scale = keep.tile([P, PACK, P], U8, name="wb_scale", tag="x_plane1", align_bytes=64)
-                nc.vector.tensor_copy(wb_scale[:], wb_scale_raw[:].rearrange("p (m t) -> p t m", t=PACK))
+
+        x_picked = keep.tile([P, PACK, J], F32, name="x_picked")
+        for j0, width in ((0, CHUNK), (CHUNK, CHUNK), (HALF, HALF)):
+            gather(x_picked[:, 0, j0 : j0 + width], x_plane[0], x_list, x_wgt, j0, width)
+        gather(x_picked[:, 1, :], x_plane[1], x_list, x_wgt, 0, J)
+        wb_scale = keep.tile([P, PACK, P], U8, name="wb_scale", tag="x_plane1", align_bytes=MX_ALIGN)
+        nc.vector.tensor_copy(wb_scale[:], wb_scale_raw[:].rearrange("p (m t) -> p t m", t=PACK))
+        gather(x_picked[:, 2, :], x_plane[2], x_list, x_wgt, 0, J)
+        for j0 in (0, HALF):
+            gather(x_picked[:, 3, j0 : j0 + HALF], x_plane[3], x_list, x_wgt, j0, HALF)
         x_grouped = []
         for h in range(2):
-            x_grouped.append(keep.tile([P, HALF, PACK], BF16, name="x_grouped%d" % h, tag="x_grouped%d" % h, align_bytes=64))
-            interleave(nc.scalar.copy, x_grouped[h][:], x_picked[h][:])
-        wa_grouped = keep.tile([P, N, PACK], BF16, name="wa_grouped", align_bytes=64)
-        wa_scales = keep.tile([P, N], U8, name="wa_scales", align_bytes=64)
+            x_grouped.append(
+                keep.tile([P, HALF, PACK], BF16, name="x_grouped%d" % h, tag="x_grouped%d" % h, align_bytes=MX_ALIGN)
+            )
+            group(nc.scalar.copy, x_grouped[h][:], x_picked[:, :, h * HALF : (h + 1) * HALF])
+
+        wa_grouped = keep.tile([P, N, PACK], BF16, name="wa_grouped", align_bytes=MX_ALIGN)
         nc.scalar.activation(
             wa_grouped[:].rearrange("p (t m) i -> p m t i", t=PACK),
             wa_raw[:].rearrange("p i (m t) -> p m t i", t=PACK),
             ACT.Copy,
             scale=-1.0,
         )
+
+        z_early = keep.tile([P, 2, J], F32, name="z_early")
+        x_scales = keep.tile([P, J], U8, name="x_scales", align_bytes=MX_ALIGN)
         x_codes = []
         for i in range(2):
-            for h in range(2):
-                gather(z_early[h][:, i, :], z_plane[i], z_list, z_wgt, h * HALF, HALF)
-            x_codes.append(keep.tile([P, HALF], U32, name="x_codes%d" % i, tag="z_plane%d" % i, align_bytes=64))
+            gather(z_early[:, i, :], z_plane[i], z_list, z_wgt, 0, J)
+            x_codes.append(keep.tile([P, HALF], U32, name="x_codes%d" % i, tag="z_plane%d" % i, align_bytes=MX_ALIGN))
             quantize(x_codes[i][:], x_scales[:, i * HALF : (i + 1) * HALF], x_grouped[i][:])
-        wa_codes = keep.tile([P, N], U32, name="wa_codes", tag="x_grouped1", align_bytes=64)
+        wa_codes = keep.tile([P, N], U32, name="wa_codes", tag="x_grouped1", align_bytes=MX_ALIGN)
+        wa_scales = keep.tile([P, N], U8, name="wa_scales", align_bytes=MX_ALIGN)
         quantize(wa_codes[:], wa_scales[:], wa_grouped[:])
+        z_grouped = []
         for c in range(CHUNKS):
-            local = slice((c % 2) * CHUNK, (c % 2 + 1) * CHUNK)
-            interleave(nc.scalar.copy, z_grouped[c][:, :, 0:2], z_early[c // 2][:, :, local])
+            z_grouped.append(
+                keep.tile([P, CHUNK, PACK], BF16, name="z_grouped%d" % c, tag="z_grouped%d" % c, align_bytes=MX_ALIGN)
+            )
+            group(nc.scalar.copy, z_grouped[c][:, :, 0:2], z_early[:, :, chunk(c)])
 
-        banks = [[psum.tile([P, 2, CHUNK], F32, name="sums%d_%d" % (c, h), tag="bank%d" % (2 * c + h)) for h in range(2)] for c in range(CHUNKS)]
+        sums = [
+            [psum.tile([P, 2, CHUNK], F32, name="sums%d_%d" % (c, u), tag="bank%d" % (2 * c + u)) for u in range(2)]
+            for c in range(CHUNKS)
+        ]
         for c in range(CHUNKS):
-            cols = slice(c * CHUNK, (c + 1) * CHUNK)
+            h, u = divmod(c, HALF // CHUNK)
             for t in range(PACK):
                 nc.tensor.matmul_mx(
-                    out=banks[c][t // 2][:, t % 2, :],
+                    out=sums[c][t // 2][:, t % 2, :],
                     lhsT=wa_codes[:, t * P : (t + 1) * P].bitcast(FP8X4),
                     lhsT_scale=wa_scales[:, t * P : (t + 1) * P],
-                    rhs=x_codes[c // 2][:, (c % 2) * CHUNK : (c % 2 + 1) * CHUNK].bitcast(FP8X4),
-                    rhs_scale=x_scales[:, cols],
+                    rhs=x_codes[h][:, chunk(u)].bitcast(FP8X4),
+                    rhs_scale=x_scales[:, chunk(c)],
                     start=(t % 2 == 0),
                     stop=False,
                 )
 
-        y_codes = keep.tile([P, J], U32, name="y_codes", align_bytes=64)
-        y_scales = keep.tile([P, J], U8, name="y_scales", align_bytes=64)
+        z_codes = keep.tile([P, J], U32, name="z_codes", align_bytes=MX_ALIGN)
+        z_scales = keep.tile([P, J], U8, name="z_scales", align_bytes=MX_ALIGN)
+        y_codes = keep.tile([P, J], U32, name="y_codes", align_bytes=MX_ALIGN)
+        y_scales = keep.tile([P, J], U8, name="y_scales", align_bytes=MX_ALIGN)
+        distance = [keep.tile([P, PACK, CHUNK], F32, name="distance%d" % c) for c in range(CHUNKS)]
+        y = [keep.tile([P, PACK, CHUNK], F32, name="y%d" % c) for c in range(CHUNKS)]
         y_rows = out_0.rearrange("(p t) j -> p t j", t=PACK)
-        y_words = out_1[0].rearrange("p j i -> p (j i)").bitcast(I32)
+        y_words = out_1[0].rearrange("p j t -> p (j t)").bitcast(I32)
 
-        def front(c):
-            cols = slice(c * CHUNK, (c + 1) * CHUNK)
-            interleave(nc.scalar.copy, z_grouped[c][:, :, 2:PACK], z_late[c][:])
-            quantize(z_codes[:, cols], z_scales[:, cols], z_grouped[c][:])
+        def finish_sums(c, z_late):
+            group(nc.scalar.copy, z_grouped[c][:, :, 2:PACK], z_late)
+            quantize(z_codes[:, chunk(c)], z_scales[:, chunk(c)], z_grouped[c][:])
             for t in range(PACK):
                 for s in range(CHUNK // FP4_N):
                     part = slice(c * CHUNK + s * FP4_N, c * CHUNK + (s + 1) * FP4_N)
                     nc.tensor.matmul_mx(
-                        out=banks[c][t // 2][:, t % 2, s * FP4_N : (s + 1) * FP4_N],
+                        out=sums[c][t // 2][:, t % 2, s * FP4_N : (s + 1) * FP4_N],
                         lhsT=wb_codes[:, t, :].bitcast(FP4X4),
                         lhsT_scale=wb_scale[:, t, :],
                         rhs=z_codes[:, part].bitcast(FP8X4),
@@ -199,49 +208,37 @@ def tile_list_absd_biasP_kernel(
                         stop=(t % 2 == 1 and s == CHUNK // FP4_N - 1),
                     )
 
-        dist = [keep.tile([P, PACK, CHUNK], F32, name="dist%d" % c) for c in range(CHUNKS)]
-        y = [keep.tile([P, PACK, CHUNK], F32, name="y%d" % c) for c in range(CHUNKS)]
+        def store_result(c):
+            for u in range(2):
+                pair = slice(2 * u, 2 * u + 2)
+                nc.scalar.activation(distance[c][:, pair, :], sums[c][u][:], ACT.Abs)
+                for t in range(pair.start, pair.stop):
+                    nc.vector.tensor_scalar_add(y[c][:, t, :], distance[c][:, t, :], bias[:, t : t + 1])
+                nc.sync.dma_start(y_rows[:, pair, chunk(c)], y[c][:, pair, :])
 
-        def distance(c):
-            for h in range(2):
-                nc.scalar.activation(dist[c][:, 2 * h : 2 * h + 2, :], banks[c][h][:], ACT.Abs)
-
-        def add_bias(c):
-            for t in range(PACK):
-                nc.vector.tensor_scalar_add(y[c][:, t, :], dist[c][:, t, :], bias[:, t : t + 1])
-            nc.sync.dma_start(y_rows[:, :, c * CHUNK : (c + 1) * CHUNK], y[c][:])
-
-        def hand_on(c):
-            cols = slice(c * CHUNK, (c + 1) * CHUNK)
-            y_grouped = keep.tile([P, CHUNK, PACK], BF16, name="y_grouped%d" % c, align_bytes=64)
-            interleave(nc.scalar.copy if c < 2 else nc.vector.tensor_copy, y_grouped[:], y[c][:])
-            quantize(y_codes[:, cols], y_scales[:, cols], y_grouped[:])
-            nc.sync.dma_start(y_words[:, cols], y_codes[:, cols].bitcast(I32))
-
-        z_late = []
-
-        def late_gathers(c, planes):
-            if len(z_late) == c:
-                tag = "z_late%d" % c if c < 2 else "z_grouped%d" % (c - 2)
-                z_late.append(keep.tile([P, 2, CHUNK], F32, name="z_late%d" % c, tag=tag, align_bytes=64))
-            for i in planes:
-                gather(z_late[c][:, i - 2, :], z_plane[i], z_list, z_wgt, c * CHUNK, CHUNK)
-
-        for i in (2, 3):
-            for c in range(2):
-                late_gathers(c, [i])
-        front(0)
-        front(1)
+        z_first = keep.tile([P, 2, AHEAD * CHUNK], F32, name="z_first")
+        gather(z_first[:, 0, :], z_plane[2], z_list, z_wgt, 0, AHEAD * CHUNK)
+        for c in range(AHEAD):
+            gather(z_first[:, 1, chunk(c)], z_plane[3], z_list, z_wgt, c * CHUNK, CHUNK)
+        for c in range(AHEAD):
+            finish_sums(c, z_first[:, :, chunk(c)])
         for c in range(CHUNKS):
-            distance(c)
-            add_bias(c)
-            if c + 2 < CHUNKS:
-                late_gathers(c + 2, [2, 3])
-                front(c + 2)
+            store_result(c)
+            later = c + AHEAD
+            if later < CHUNKS:
+                z_late = keep.tile([P, 2, CHUNK], F32, name="z_late", tag="z_grouped%d" % c, align_bytes=MX_ALIGN)
+                for i in range(2, PACK):
+                    gather(z_late[:, i - 2, :], z_plane[i], z_list, z_wgt, later * CHUNK, CHUNK)
+                finish_sums(later, z_late[:])
+
         for c in range(CHUNKS):
-            hand_on(c)
-        for q in range(4):
-            eng = nc.sync if q % 2 == 0 else nc.scalar
-            eng.dma_start(
-                out_2[0, 4 * q : 4 * q + 4, :].bitcast(I32), y_scales[32 * q : 32 * q + 4, :].bitcast(I32)
+            y_grouped = keep.tile([P, CHUNK, PACK], BF16, name="y_grouped%d" % c, align_bytes=MX_ALIGN)
+            group(nc.scalar.copy if c < SCALAR_ROUNDS else nc.vector.tensor_copy, y_grouped[:], y[c][:])
+            quantize(y_codes[:, chunk(c)], y_scales[:, chunk(c)], y_grouped[:])
+            nc.sync.dma_start(y_words[:, chunk(c)], y_codes[:, chunk(c)].bitcast(I32))
+        for q in range(P // QUADRANT):
+            queue = nc.sync if q % 2 == 0 else nc.scalar
+            queue.dma_start(
+                out_2[0, SCALE_ROWS * q : SCALE_ROWS * (q + 1), :].bitcast(I32),
+                y_scales[QUADRANT * q : QUADRANT * q + SCALE_ROWS, :].bitcast(I32),
             )

from contextlib import ExitStack

import concourse.mybir as mybir
from concourse.masks import make_identity

K, L, N, T, J = 512, 512, 512, 2048, 1024
FLOPS = 2 * (K + L) * N * J

F32 = mybir.dt.float32
BF16 = mybir.dt.bfloat16
I32 = mybir.dt.int32
U32 = mybir.dt.uint32
U16 = mybir.dt.uint16
U8 = mybir.dt.uint8
FP8X4 = mybir.dt.float8_e4m3fn_x4
FP4X4 = mybir.dt.float4_e2m1fn_x4
ACT = mybir.ActivationFunctionType

P = 128
PACK = 4
HEADS = 8
LANES = P // HEADS
QUADRANT = 32
SCALE_ROWS = 4
HALF = J // 2
CHUNK = 256
CHUNKS = J // CHUNK
FP4_N = 128
MX_ALIGN = 64
AHEAD = 3
SCALAR_ROUNDS = 2


def tile_list_absd_biasP_kernel(
    tc, xT, wgt, zT, wgt2, wa, wb_words, wb_scales, b, offs, offs2, out_0, out_1, out_2
):
    nc = tc.nc
    with ExitStack() as ctx:
        keep = ctx.enter_context(tc.tile_pool(name="keep", bufs=1))
        psum = ctx.enter_context(tc.psum_pool(name="psum", bufs=1))

        def group(copy, grouped, planes):
            copy(
                grouped.rearrange("p (c e) i -> p c i e", e=4),
                planes.rearrange("p i (c e) -> p c i e", e=4),
            )

        def quantize(codes, scales, grouped):
            nc.vector.quantize_mx(out=codes.bitcast(FP8X4), scales=scales, in_=grouped.rearrange("p j i -> p (j i)"))

        def gather(picked, plane, lists, weights, j0, width):
            nc.vector.tensor_tensor(
                picked,
                plane[:].indirect(lists[:, j0 // LANES : (j0 + width) // LANES]),
                weights[:, j0 : j0 + width],
                mybir.AluOpType.mult,
            )

        def chunk(c):
            return slice(c * CHUNK, (c + 1) * CHUNK)

        x_plane = [keep.tile([P, T], F32, name="x_plane%d" % i, tag="x_plane%d" % i, align_bytes=MX_ALIGN) for i in range(PACK)]
        z_plane = [keep.tile([P, T], F32, name="z_plane%d" % i, tag="z_plane%d" % i, align_bytes=MX_ALIGN) for i in range(PACK)]
        x_list = keep.tile([P, J // LANES], U16, name="x_list")
        z_list = keep.tile([P, J // LANES], U16, name="z_list")
        wgt_rows = keep.tile([P, HALF], F32, name="wgt_rows")
        wa_raw = keep.tile([P, PACK, N], F32, name="wa_raw")
        wb_raw = keep.tile([P, 2 * N], U8, name="wb_raw")
        wb_scale_raw = keep.tile([P, N], U8, name="wb_scale_raw")
        bias = keep.tile([P, PACK], F32, name="bias")
        identity = keep.tile([P, P], F32, name="identity")

        nc.gpsimd.memset(wb_scale_raw[:].bitcast(I32), 0)
        nc.vector.memset(wgt_rows[QUADRANT : 2 * QUADRANT, :], 0.0)
        nc.vector.memset(wgt_rows[2 * QUADRANT :, :], 0.0)
        make_identity(nc, identity[:])

        x_rows = xT.rearrange("(p i) t -> p i t", i=PACK)
        z_rows = zT.rearrange("(p i) t -> p i t", i=PACK)
        step = LANES + 1
        nc.sync.dma_start(wgt_rows[: 2 * HEADS, :], wgt.rearrange("p (h j) -> (p h) j", h=2)[0 : 2 * P : step, :])
        nc.scalar.dma_start(
            wgt_rows[2 * HEADS : 4 * HEADS, :], wgt2.rearrange("p (h j) -> (p h) j", h=2)[0 : 2 * P : step, :]
        )
        nc.scalar.dma_start(wb_raw[:].bitcast(I32), wb_words[0].bitcast(I32))
        nc.sync.dma_start(x_list[:], offs)
        nc.sync.dma_start(x_plane[0][:], x_rows[:, 0, :])
        for q in range(P // QUADRANT):
            nc.sync.dma_start(
                wb_scale_raw[QUADRANT * q : QUADRANT * q + SCALE_ROWS, :].bitcast(I32),
                wb_scales[0, SCALE_ROWS * q : SCALE_ROWS * (q + 1), :].bitcast(I32),
            )
        for i in range(1, PACK):
            nc.sync.dma_start(x_plane[i][:], x_rows[:, i, :])
        nc.sync.dma_start(z_list[:], offs2)
        nc.sync.dma_start(bias[:], b.rearrange("(p t) -> p t", t=PACK))
        nc.sync.dma_start(z_plane[0][:], z_rows[:, 0, :])
        nc.sync.dma_start(wa_raw[:], wa.rearrange("(p i) n -> p i n", i=PACK))
        for i in range(1, PACK):
            nc.sync.dma_start(z_plane[i][:], z_rows[:, i, :])

        x_wgt = keep.tile([P, J], F32, name="x_wgt")
        z_wgt = keep.tile([P, J], F32, name="z_wgt")
        blocks = CHUNK // P
        turned = []
        for u in range(HALF // CHUNK):
            turned.append(psum.tile([P, blocks, P], F32, name="turned%d" % u, tag="bank%d" % u))
            for s in range(blocks):
                first = u * CHUNK + s * P
                nc.tensor.transpose(turned[u][:, s, :], wgt_rows[:, first : first + P], identity[:])
        for w, weights in enumerate((x_wgt, z_wgt)):
            for c in range(CHUNKS):
                h, u = divmod(c, HALF // CHUNK)
                heads = turned[u][:, :, 2 * HEADS * w + h : 2 * HEADS * (w + 1) + h - 1 : 2]
                repeated = keep.tile([P, blocks, HEADS, LANES], F32, name="repeated", bufs=CHUNKS)
                nc.scalar.copy(repeated[:], heads.unsqueeze(3).to_broadcast([P, blocks, HEADS, LANES]))
                spread = psum.tile([P, blocks, P], F32, name="spread", tag="bank%d" % (len(turned) + c))
                for s in range(blocks):
                    nc.tensor.transpose(spread[:, s, :], repeated[:, s, :, :].rearrange("p g r -> p (g r)"), identity[:])
                nc.scalar.copy(weights[:, chunk(c)], spread[:].rearrange("p s j -> p (s j)"))

        wb_codes = keep.tile([P, PACK, 2 * P], U8, name="wb_codes", align_bytes=MX_ALIGN)
        nc.vector.tensor_copy(
            wb_codes[:].rearrange("p t (m e) -> p t m e", e=2),
            wb_raw[:].rearrange("p (m t e) -> p t m e", t=PACK, e=2),
        )

        x_picked = keep.tile([P, PACK, J], F32, name="x_picked")
        for j0, width in ((0, CHUNK), (CHUNK, CHUNK), (HALF, HALF)):
            gather(x_picked[:, 0, j0 : j0 + width], x_plane[0], x_list, x_wgt, j0, width)
        gather(x_picked[:, 1, :], x_plane[1], x_list, x_wgt, 0, J)
        wb_scale = keep.tile([P, PACK, P], U8, name="wb_scale", tag="x_plane1", align_bytes=MX_ALIGN)
        nc.vector.tensor_copy(wb_scale[:], wb_scale_raw[:].rearrange("p (m t) -> p t m", t=PACK))
        gather(x_picked[:, 2, :], x_plane[2], x_list, x_wgt, 0, J)
        for j0 in (0, HALF):
            gather(x_picked[:, 3, j0 : j0 + HALF], x_plane[3], x_list, x_wgt, j0, HALF)
        x_grouped = []
        for h in range(2):
            x_grouped.append(
                keep.tile([P, HALF, PACK], BF16, name="x_grouped%d" % h, tag="x_grouped%d" % h, align_bytes=MX_ALIGN)
            )
            group(nc.scalar.copy, x_grouped[h][:], x_picked[:, :, h * HALF : (h + 1) * HALF])

        wa_grouped = keep.tile([P, N, PACK], BF16, name="wa_grouped", align_bytes=MX_ALIGN)
        nc.scalar.activation(
            wa_grouped[:].rearrange("p (t m) i -> p m t i", t=PACK),
            wa_raw[:].rearrange("p i (m t) -> p m t i", t=PACK),
            ACT.Copy,
            scale=-1.0,
        )

        z_early = keep.tile([P, 2, J], F32, name="z_early")
        x_scales = keep.tile([P, J], U8, name="x_scales", align_bytes=MX_ALIGN)
        x_codes = []
        for i in range(2):
            gather(z_early[:, i, :], z_plane[i], z_list, z_wgt, 0, J)
            x_codes.append(keep.tile([P, HALF], U32, name="x_codes%d" % i, tag="z_plane%d" % i, align_bytes=MX_ALIGN))
            quantize(x_codes[i][:], x_scales[:, i * HALF : (i + 1) * HALF], x_grouped[i][:])
        wa_codes = keep.tile([P, N], U32, name="wa_codes", tag="x_grouped1", align_bytes=MX_ALIGN)
        wa_scales = keep.tile([P, N], U8, name="wa_scales", align_bytes=MX_ALIGN)
        quantize(wa_codes[:], wa_scales[:], wa_grouped[:])
        z_grouped = []
        for c in range(CHUNKS):
            z_grouped.append(
                keep.tile([P, CHUNK, PACK], BF16, name="z_grouped%d" % c, tag="z_grouped%d" % c, align_bytes=MX_ALIGN)
            )
            group(nc.scalar.copy, z_grouped[c][:, :, 0:2], z_early[:, :, chunk(c)])

        sums = [
            [psum.tile([P, 2, CHUNK], F32, name="sums%d_%d" % (c, u), tag="bank%d" % (2 * c + u)) for u in range(2)]
            for c in range(CHUNKS)
        ]
        for c in range(CHUNKS):
            h, u = divmod(c, HALF // CHUNK)
            for t in range(PACK):
                nc.tensor.matmul_mx(
                    out=sums[c][t // 2][:, t % 2, :],
                    lhsT=wa_codes[:, t * P : (t + 1) * P].bitcast(FP8X4),
                    lhsT_scale=wa_scales[:, t * P : (t + 1) * P],
                    rhs=x_codes[h][:, chunk(u)].bitcast(FP8X4),
                    rhs_scale=x_scales[:, chunk(c)],
                    start=(t % 2 == 0),
                    stop=False,
                )

        z_codes = keep.tile([P, J], U32, name="z_codes", align_bytes=MX_ALIGN)
        z_scales = keep.tile([P, J], U8, name="z_scales", align_bytes=MX_ALIGN)
        y_codes = keep.tile([P, J], U32, name="y_codes", align_bytes=MX_ALIGN)
        y_scales = keep.tile([P, J], U8, name="y_scales", align_bytes=MX_ALIGN)
        distance = [keep.tile([P, PACK, CHUNK], F32, name="distance%d" % c) for c in range(CHUNKS)]
        y = [keep.tile([P, PACK, CHUNK], F32, name="y%d" % c) for c in range(CHUNKS)]
        y_rows = out_0.rearrange("(p t) j -> p t j", t=PACK)
        y_words = out_1[0].rearrange("p j t -> p (j t)").bitcast(I32)

        def finish_sums(c, z_late):
            group(nc.scalar.copy, z_grouped[c][:, :, 2:PACK], z_late)
            quantize(z_codes[:, chunk(c)], z_scales[:, chunk(c)], z_grouped[c][:])
            for t in range(PACK):
                for s in range(CHUNK // FP4_N):
                    part = slice(c * CHUNK + s * FP4_N, c * CHUNK + (s + 1) * FP4_N)
                    nc.tensor.matmul_mx(
                        out=sums[c][t // 2][:, t % 2, s * FP4_N : (s + 1) * FP4_N],
                        lhsT=wb_codes[:, t, :].bitcast(FP4X4),
                        lhsT_scale=wb_scale[:, t, :],
                        rhs=z_codes[:, part].bitcast(FP8X4),
                        rhs_scale=z_scales[:, part],
                        start=False,
                        stop=(t % 2 == 1 and s == CHUNK // FP4_N - 1),
                    )

        def store_result(c):
            for u in range(2):
                pair = slice(2 * u, 2 * u + 2)
                nc.scalar.activation(distance[c][:, pair, :], sums[c][u][:], ACT.Abs)
                for t in range(pair.start, pair.stop):
                    nc.vector.tensor_scalar_add(y[c][:, t, :], distance[c][:, t, :], bias[:, t : t + 1])
                nc.sync.dma_start(y_rows[:, pair, chunk(c)], y[c][:, pair, :])

        z_first = keep.tile([P, 2, AHEAD * CHUNK], F32, name="z_first")
        gather(z_first[:, 0, :], z_plane[2], z_list, z_wgt, 0, AHEAD * CHUNK)
        for c in range(AHEAD):
            gather(z_first[:, 1, chunk(c)], z_plane[3], z_list, z_wgt, c * CHUNK, CHUNK)
        for c in range(AHEAD):
            finish_sums(c, z_first[:, :, chunk(c)])
        for c in range(CHUNKS):
            store_result(c)
            later = c + AHEAD
            if later < CHUNKS:
                z_late = keep.tile([P, 2, CHUNK], F32, name="z_late", tag="z_grouped%d" % c, align_bytes=MX_ALIGN)
                for i in range(2, PACK):
                    gather(z_late[:, i - 2, :], z_plane[i], z_list, z_wgt, later * CHUNK, CHUNK)
                finish_sums(later, z_late[:])

        for c in range(CHUNKS):
            y_grouped = keep.tile([P, CHUNK, PACK], BF16, name="y_grouped%d" % c, align_bytes=MX_ALIGN)
            group(nc.scalar.copy if c < SCALAR_ROUNDS else nc.vector.tensor_copy, y_grouped[:], y[c][:])
            quantize(y_codes[:, chunk(c)], y_scales[:, chunk(c)], y_grouped[:])
            nc.sync.dma_start(y_words[:, chunk(c)], y_codes[:, chunk(c)].bitcast(I32))
        for q in range(P // QUADRANT):
            queue = nc.sync if q % 2 == 0 else nc.scalar
            queue.dma_start(
                out_2[0, SCALE_ROWS * q : SCALE_ROWS * (q + 1), :].bitcast(I32),
                y_scales[QUADRANT * q : QUADRANT * q + SCALE_ROWS, :].bitcast(I32),
            )
